import numpy as np
import ml_dtypes


def mxq(x, axis, fmt="e4m3"):
    dtype, down = {"e4m3": (ml_dtypes.float8_e4m3fn, 7), "e5m2": (ml_dtypes.float8_e5m2, 14)}[fmt]
    v = np.moveaxis(np.asarray(x, np.float32).astype(ml_dtypes.bfloat16).astype(np.float64), axis, -1)
    blocks = v.reshape(v.shape[:-1] + (-1, 32))
    amax = np.abs(blocks).max(-1, keepdims=True)
    byte = np.maximum(np.where(amax > 0, np.frexp(amax)[1] - 1 + 127, 0) - down, 1)
    scale = np.exp2(byte - 127.0)
    codes = (blocks / scale).astype(np.float32).astype(dtype).astype(np.float64)
    return np.moveaxis((codes * scale).reshape(v.shape), -1, axis)


WIDE = False


def mx_kscale(k):
    if not WIDE:
        return np.ones(k)
    levels = np.array([30, -30])
    if k % 512:
        return np.exp2(np.random.permutation(np.resize(levels, k // 32))).repeat(32)
    a = np.empty((k // 512, 16))
    for p in range(k // 512):
        a[p, :8] = np.random.permutation(np.resize(levels, 8))
        for g in range(8):
            far = levels[np.abs(levels - a[p, g]) >= 10]
            a[p, g + 8] = far[np.random.randint(len(far))]
    return np.exp2(a.ravel()).repeat(32)


def f64(x):
    return np.asarray(x).astype(np.float64)


def striped(idx):
    return np.tile(np.asarray(idx).reshape(-1, 16).T, (8, 1)).astype(np.uint16)


def unstriped(offs):
    return offs[:16].T.reshape(-1).astype(np.int64)


E2M1 = np.array([0.0, 0.5, 1.0, 1.5, 2.0, 3.0, 4.0, 6.0, -0.0, -0.5, -1.0, -1.5, -2.0, -3.0, -4.0, -6.0])


def pack_weight(w, fmt):
    k, n = w.shape
    w = f64(np.asarray(w, np.float32).astype(ml_dtypes.bfloat16)).reshape(k // 32, 32, n)
    amax = np.abs(w).max(1)
    if fmt == "e4m3":
        byte = np.frexp(amax)[1] - 1 + 127 - 7
    else:
        mant, ex = np.frexp(amax / 6.0)
        byte = np.where(mant > 0.5, ex, ex - 1) + 127
    byte = np.clip(np.where(amax > 0, byte, 1), 1, 254)
    scaled = (w * np.exp2(127.0 - byte)[:, None, :]).reshape(k, n).astype(np.float32)
    by_word = np.ascontiguousarray(scaled.reshape(k // 512, 128, 4, n).transpose(0, 1, 3, 2))
    if fmt == "e4m3":
        words = by_word.astype(ml_dtypes.float8_e4m3fn).view(np.uint8)
    else:
        c = by_word.astype(ml_dtypes.float4_e2m1fn).view(np.uint8) & 0xF
        words = (c[..., 0::2] | (c[..., 1::2] << 4)).reshape(k // 512, 128, 2 * n)
    return np.ascontiguousarray(words), np.ascontiguousarray(byte.astype(np.uint8).reshape(k // 512, 16, n))


def unpack_weight(words, scales, fmt):
    g, _, n = scales.shape
    words = np.ascontiguousarray(words).reshape(g, 128, n, -1)
    if fmt == "e4m3":
        vals = words.view(ml_dtypes.float8_e4m3fn).astype(np.float64)
    else:
        nib = np.empty((g, 128, n, 4), np.uint8)
        nib[..., 0::2] = words & 0xF
        nib[..., 1::2] = words >> 4
        vals = E2M1[nib]
    vals = vals * np.repeat(np.exp2(scales.astype(np.float64) - 127.0), 8, axis=1)[..., None]
    return vals.transpose(0, 1, 3, 2).reshape(g * 512, n)


K, T, J, R, O, N, L, E = 512, 2048, 256, 512, 128, 256, 512, 1024


def setup_inputs():
    n = np.random.standard_normal
    idx = np.random.permutation(T)[:J]
    idx2 = np.random.permutation(T)[:J]
    idx3 = np.random.permutation(J)[:O]
    idx4 = np.random.permutation(J)[:O]
    idx5 = np.random.permutation(E)[:O]
    fk = mx_kscale(K)
    fr = mx_kscale(R)
    fl = mx_kscale(L)
    xtp = pack_weight(n((K, T)) / fk[:, None], "e2m1")
    wp = pack_weight(n((K, R)) * 1 / np.sqrt(K) * fk[:, None] * fr, "e4m3")
    wbp = pack_weight(n((R, N)) * 1 / np.sqrt(R) / fr[:, None], "e2m1")
    sxp = pack_weight(n((L, O)) / fl[:, None], "e4m3")
    wsp = pack_weight(n((L, N)) * 1 / np.sqrt(L) * fl[:, None], "e4m3")
    return {
        "xt_words": xtp[0],
        "xt_scales": xtp[1],
        "w_words": wp[0],
        "w_scales": wp[1],
        "wb_words": wbp[0],
        "wb_scales": wbp[1],
        "sx_words": sxp[0],
        "sx_scales": sxp[1],
        "ws_words": wsp[0],
        "ws_scales": wsp[1],
        "offs": striped(idx),
        "offs2": striped(idx2),
        "offs3": striped(idx3),
        "offs4": striped(idx4),
        "offs5": striped(idx5),
    }


def reference(xt_words, xt_scales, w_words, w_scales, wb_words, wb_scales, sx_words, sx_scales, ws_words, ws_scales, offs, offs2, offs3, offs4, offs5):
    idx = unstriped(offs)
    idx2 = unstriped(offs2)
    idx3 = unstriped(offs3)
    idx4 = unstriped(offs4)
    idx5 = unstriped(offs5)
    xtu = unpack_weight(xt_words, xt_scales, "e2m1")
    wu = unpack_weight(w_words, w_scales, "e4m3")
    wbu = unpack_weight(wb_words, wb_scales, "e2m1")
    sxu = unpack_weight(sx_words, sx_scales, "e4m3")
    wsu = unpack_weight(ws_words, ws_scales, "e4m3")
    xtidxg = xtu[:, idx]
    a = wu.T @ xtidxg
    xtidx2g = xtu[:, idx2]
    b = wu.T @ xtidx2g
    hid = np.abs(a[:, idx3] - b[:, idx4])
    hidq = mxq(hid, 0, "e5m2")
    p = wbu.T @ hidq + wsu.T @ sxu
    y = np.zeros((N, E))
    y[:, idx5] = p
    return y

@@ -1,0 +1,157 @@
+from contextlib import ExitStack
+
+import concourse.mybir as mybir
+
+K, T, J, R, O, N, L, E = 512, 2048, 256, 512, 128, 256, 512, 1024
+FLOPS = 2 * (2 * K * R * J + R * N * O + L * N * O)
+
+F32 = mybir.dt.float32
+BF16 = mybir.dt.bfloat16
+I32 = mybir.dt.int32
+U32 = mybir.dt.uint32
+U16 = mybir.dt.uint16
+U8 = mybir.dt.uint8
+E4M3 = mybir.dt.float8_e4m3fn_x4
+E5M2 = mybir.dt.float8_e5m2_x4
+E2M1 = mybir.dt.float4_e2m1fn_x4
+ACT = mybir.ActivationFunctionType
+ALU = mybir.AluOpType
+
+P = 128
+PACK = 4
+QUADS = 4
+
+
+def tile_list_tied_looked_skip_scattered_kernel(
+    tc, xt_words, xt_scales, w_words, w_scales, wb_words, wb_scales, sx_words, sx_scales,
+    ws_words, ws_scales, offs, offs2, offs3, offs4, offs5, out,
+):
+    nc = tc.nc
+    with ExitStack() as ctx:
+        sb = ctx.enter_context(tc.tile_pool(name="sb", bufs=1))
+        ps = ctx.enter_context(tc.psum_pool(name="ps", bufs=1))
+
+        def tile(name, cols, dtype):
+            return sb.tile([P, cols], dtype, name=name, align_bytes=64)
+
+        def load_list(name, src):
+            t = tile(name, src.shape[1], U16)
+            nc.sync.dma_start(t[:], src)
+            return t
+
+        def load_scale_rows(queue, plane, src, q):
+            queue.dma_start(plane[32 * q : 32 * q + 4, :].bitcast(I32), src[0, 4 * q : 4 * q + 4, :].bitcast(I32))
+
+        def words_i32(src):
+            return src[0].rearrange("p n t -> p (n t)").bitcast(I32)
+
+        xt_w = tile("xt_w", T, U16)
+        xt_s = tile("xt_s", T, U8)
+        w_raw = tile("w_raw", R, U32)
+        w_s_raw = tile("w_s_raw", R, U8)
+        late_s = tile("late_s", 2 * N + O, U8)
+        wb_s, ws_s, sx_s = late_s[:, 0:N], late_s[:, N : 2 * N], late_s[:, 2 * N : 2 * N + O]
+        wb_w = tile("wb_w", 2 * N, U8)
+        ws_w = tile("ws_w", N, U32)
+        sx_w = tile("sx_w", O, U32)
+        pages = [tile("page%d" % h, E, F32) for h in range(2)]
+
+        nc.vector.memset(w_s_raw[:].bitcast(I32), 0)
+        nc.vector.memset(xt_s[:].bitcast(I32), 0)
+        nc.vector.memset(late_s[:].bitcast(I32), 0)
+        for page in pages:
+            nc.vector.memset(page[:], 0.0)
+
+        l1 = load_list("l1", offs)
+        l2 = load_list("l2", offs2)
+        for q in range(QUADS):
+            load_scale_rows(nc.sync, w_s_raw, w_scales, q)
+        nc.sync.dma_start(xt_w[:].bitcast(I32), xt_words[0].bitcast(I32))
+        nc.sync.dma_start(w_raw[:].bitcast(I32), words_i32(w_words))
+        for q in range(QUADS):
+            load_scale_rows(nc.sync, xt_s, xt_scales, q)
+        l3 = load_list("l3", offs3)
+        l4 = load_list("l4", offs4)
+        nc.sync.dma_start(ws_w[:].bitcast(I32), words_i32(ws_words))
+        nc.sync.dma_start(sx_w[:].bitcast(I32), words_i32(sx_words))
+        for q in range(QUADS):
+            load_scale_rows(nc.gpsimd, sx_s, sx_scales, q)
+        for q in range(QUADS):
+            load_scale_rows(nc.sync, ws_s, ws_scales, q)
+        nc.sync.dma_start(wb_w[:].bitcast(I32), wb_words[0].bitcast(I32))
+        for q in range(QUADS):
+            load_scale_rows(nc.sync, wb_s, wb_scales, q)
+        l5 = load_list("l5", offs5)
+
+        w_w = tile("w_w", R, U32)
+        w_s = tile("w_s", R, U8)
+        picked_w = [tile("picked_w%d" % i, J, U16) for i in range(2)]
+        picked_s = [tile("picked_s%d" % i, J, U8) for i in range(2)]
+
+        def deal(engine, dst, src, t0, t1):
+            engine(
+                dst[:].rearrange("p (t m) -> p t m", t=PACK)[:, t0:t1, :],
+                src[:].rearrange("p (m t) -> p t m", t=PACK)[:, t0:t1, :],
+            )
+
+        deal(nc.vector.tensor_copy, w_s, w_s_raw, 0, PACK)
+        for t in range(PACK):
+            deal(nc.scalar.copy, w_w, w_raw, t, t + 1)
+        nc.vector.tensor_copy(picked_w[0][:], xt_w[:].indirect(l1[:]))
+        nc.vector.tensor_copy(picked_s[0][:], xt_s[:].indirect(l1[:]))
+        nc.vector.tensor_copy(picked_w[1][:], xt_w[:].indirect(l2[:]))
+        nc.vector.tensor_copy(picked_s[1][:], xt_s[:].indirect(l2[:]))
+
+        banks = [[ps.tile([P, J], F32, name="bank%d%d" % (i, t), tag="bank%d%d" % (i, t)) for t in range(PACK)] for i in range(2)]
+        for i in range(2):
+            for t in range(PACK):
+                cols = slice(t * P, (t + 1) * P)
+                nc.tensor.matmul_mx(
+                    out=banks[i][t][:], lhsT=w_w[:, cols].bitcast(E4M3), lhsT_scale=w_s[:, cols],
+                    rhs=picked_w[i][:].bitcast(E2M1), rhs_scale=picked_s[i][:], start=True, stop=True,
+                )
+
+        a = [tile("a%d" % t, J, F32) for t in range(PACK)]
+        b = [tile("b%d" % t, J, F32) for t in range(PACK)]
+        a_g = sb.tile([P, PACK, O], F32, name="a_g", align_bytes=64)
+        diff = sb.tile([P, PACK, O], F32, name="diff", align_bytes=64)
+        hid = sb.tile([P, O, PACK], BF16, name="hid", align_bytes=64)
+        for t in range(PACK):
+            nc.scalar.activation(a[t][:], banks[0][t][:], ACT.Copy)
+            nc.scalar.activation(a_g[:, t, :], a[t][:].indirect(l3[:]), ACT.Copy)
+        for t in range(PACK):
+            if t < 2:
+                nc.vector.tensor_copy(b[t][:], banks[1][t][:])
+            else:
+                nc.scalar.activation(b[t][:], banks[1][t][:], ACT.Copy)
+            nc.vector.tensor_tensor(diff[:, t, :], b[t][:].indirect(l4[:]), a_g[:, t, :], ALU.subtract)
+        half = O // 2
+        woven = diff[:].rearrange("p t o -> p o t")
+        nc.scalar.activation(hid[:, :half, :], woven[:, :half, :], ACT.Abs)
+        nc.vector.scalar_tensor_tensor(hid[:, half:, :], woven[:, half:, :], -1.0, woven[:, half:, :], ALU.mult, ALU.max)
+
+        hid_w = tile("hid_w", O, U32)
+        hid_s = tile("hid_s", O, U8)
+        nc.vector.quantize_mx(out=hid_w[:].bitcast(E5M2), scales=hid_s[:], in_=hid[:].rearrange("p o t -> p (o t)"))
+
+        acc = [ps.tile([P, O], F32, name="acc%d" % h, tag="bank0%d" % h) for h in range(2)]
+        for h in range(2):
+            cols = slice(h * P, (h + 1) * P)
+            nc.tensor.matmul_mx(
+                out=acc[h][:], lhsT=ws_w[:, cols].bitcast(E4M3), lhsT_scale=ws_s[:, cols],
+                rhs=sx_w[:].bitcast(E4M3), rhs_scale=sx_s, start=True, stop=False,
+            )
+        for h in range(2):
+            cols = slice(h * P, (h + 1) * P)
+            nc.tensor.matmul_mx(
+                out=acc[h][:], lhsT=wb_w[:, 2 * h * P : 2 * (h + 1) * P].bitcast(E2M1), lhsT_scale=wb_s[:, cols],
+                rhs=hid_w[:].bitcast(E5M2), rhs_scale=hid_s[:], start=False, stop=True,
+            )
+
+        p_sb = [tile("p%d" % h, O, F32) for h in range(2)]
+        nc.vector.tensor_copy(p_sb[0][:], acc[0][:])
+        nc.scalar.activation(p_sb[1][:], acc[1][:], ACT.Copy)
+        nc.vector.tensor_copy(pages[0][:].indirect(l5[:]), p_sb[0][:])
+        nc.scalar.activation(pages[1][:].indirect(l5[:]), p_sb[1][:], ACT.Copy)
+        nc.sync.dma_start(out[0:P, :], pages[0][:])
+        nc.scalar.dma_start(out[P : 2 * P, :], pages[1][:])

@@ -56,8 +56,9 @@ def tile_list_tied_looked_skip_scattered_kernel(
         sx_w = tile("sx_w", O, U32)
         pages = [tile("page%d" % h, E, F32) for h in range(2)]
 
+        nc.vector.memset(xt_s[:, : T // 2].bitcast(I32), 0)
+        nc.gpsimd.memset(xt_s[:, T // 2 :].bitcast(I32), 0)
         nc.vector.memset(w_s_raw[:].bitcast(I32), 0)
-        nc.vector.memset(xt_s[:].bitcast(I32), 0)
         nc.vector.memset(late_s[:].bitcast(I32), 0)
         for page in pages:
             nc.vector.memset(page[:], 0.0)
@@ -65,17 +66,17 @@ def tile_list_tied_looked_skip_scattered_kernel(
         l1 = load_list("l1", offs)
         l2 = load_list("l2", offs2)
         for q in range(QUADS):
-            load_scale_rows(nc.sync, w_s_raw, w_scales, q)
+            load_scale_rows(nc.sync, xt_s, xt_scales, q)
+        l3 = load_list("l3", offs3)
         nc.sync.dma_start(xt_w[:].bitcast(I32), xt_words[0].bitcast(I32))
         nc.sync.dma_start(w_raw[:].bitcast(I32), words_i32(w_words))
         for q in range(QUADS):
-            load_scale_rows(nc.sync, xt_s, xt_scales, q)
-        l3 = load_list("l3", offs3)
+            load_scale_rows(nc.sync, w_s_raw, w_scales, q)
         l4 = load_list("l4", offs4)
         nc.sync.dma_start(ws_w[:].bitcast(I32), words_i32(ws_words))
         nc.sync.dma_start(sx_w[:].bitcast(I32), words_i32(sx_words))
         for q in range(QUADS):
-            load_scale_rows(nc.gpsimd, sx_s, sx_scales, q)
+            load_scale_rows(nc.sync, sx_s, sx_scales, q)
         for q in range(QUADS):
             load_scale_rows(nc.sync, ws_s, ws_scales, q)
         nc.sync.dma_start(wb_w[:].bitcast(I32), wb_words[0].bitcast(I32))
@@ -94,17 +95,18 @@ def tile_list_tied_looked_skip_scattered_kernel(
                 src[:].rearrange("p (m t) -> p t m", t=PACK)[:, t0:t1, :],
             )
 
-        deal(nc.vector.tensor_copy, w_s, w_s_raw, 0, PACK)
+        nc.vector.tensor_copy(picked_s[0][:], xt_s[:].indirect(l1[:]))
+        nc.vector.tensor_copy(picked_s[1][:], xt_s[:].indirect(l2[:]))
+        nc.vector.tensor_copy(picked_w[0][:], xt_w[:].indirect(l1[:]))
+        nc.vector.tensor_copy(picked_w[1][:], xt_w[:].indirect(l2[:]))
         for t in range(PACK):
             deal(nc.scalar.copy, w_w, w_raw, t, t + 1)
-        nc.vector.tensor_copy(picked_w[0][:], xt_w[:].indirect(l1[:]))
-        nc.vector.tensor_copy(picked_s[0][:], xt_s[:].indirect(l1[:]))
-        nc.vector.tensor_copy(picked_w[1][:], xt_w[:].indirect(l2[:]))
-        nc.vector.tensor_copy(picked_s[1][:], xt_s[:].indirect(l2[:]))
+        deal(nc.vector.tensor_copy, w_s, w_s_raw, 0, 1)
+        deal(nc.vector.tensor_copy, w_s, w_s_raw, 1, PACK)
 
         banks = [[ps.tile([P, J], F32, name="bank%d%d" % (i, t), tag="bank%d%d" % (i, t)) for t in range(PACK)] for i in range(2)]
-        for i in range(2):
-            for t in range(PACK):
+        for t in range(PACK):
+            for i in range(2):
                 cols = slice(t * P, (t + 1) * P)
                 nc.tensor.matmul_mx(
                     out=banks[i][t][:], lhsT=w_w[:, cols].bitcast(E4M3), lhsT_scale=w_s[:, cols],
@@ -116,19 +118,20 @@ def tile_list_tied_looked_skip_scattered_kernel(
         a_g = sb.tile([P, PACK, O], F32, name="a_g", align_bytes=64)
         diff = sb.tile([P, PACK, O], F32, name="diff", align_bytes=64)
         hid = sb.tile([P, O, PACK], BF16, name="hid", align_bytes=64)
+        woven = diff[:].rearrange("p t o -> p o t")
         for t in range(PACK):
             nc.scalar.activation(a[t][:], banks[0][t][:], ACT.Copy)
-            nc.scalar.activation(a_g[:, t, :], a[t][:].indirect(l3[:]), ACT.Copy)
-        for t in range(PACK):
-            if t < 2:
+            if t == 0:
                 nc.vector.tensor_copy(b[t][:], banks[1][t][:])
             else:
                 nc.scalar.activation(b[t][:], banks[1][t][:], ACT.Copy)
+            if t in (0, PACK - 1):
+                nc.scalar.activation(a_g[:, t, :], a[t][:].indirect(l3[:]), ACT.Copy)
+            else:
+                nc.vector.tensor_copy(a_g[:, t, :], a[t][:].indirect(l3[:]))
             nc.vector.tensor_tensor(diff[:, t, :], b[t][:].indirect(l4[:]), a_g[:, t, :], ALU.subtract)
-        half = O // 2
-        woven = diff[:].rearrange("p t o -> p o t")
-        nc.scalar.activation(hid[:, :half, :], woven[:, :half, :], ACT.Abs)
-        nc.vector.scalar_tensor_tensor(hid[:, half:, :], woven[:, half:, :], -1.0, woven[:, half:, :], ALU.mult, ALU.max)
+        for t in range(0, PACK, 2):
+            nc.scalar.activation(hid[:, :, t : t + 2], woven[:, :, t : t + 2], ACT.Abs)
 
         hid_w = tile("hid_w", O, U32)
         hid_s = tile("hid_s", O, U8)

@@ -20,6 +20,8 @@ ALU = mybir.AluOpType
 P = 128
 PACK = 4
 QUADS = 4
+ROW_TILES = N // P
+A, B = 0, 1
 
 
 def tile_list_tied_looked_skip_scattered_kernel(
@@ -35,126 +37,142 @@ def tile_list_tied_looked_skip_scattered_kernel(
             return sb.tile([P, cols], dtype, name=name, align_bytes=64)
 
         def load_list(name, src):
-            t = tile(name, src.shape[1], U16)
-            nc.sync.dma_start(t[:], src)
-            return t
+            offsets = tile(name, src.shape[1], U16)
+            nc.sync.dma_start(offsets[:], src)
+            return offsets
 
-        def load_scale_rows(queue, plane, src, q):
-            queue.dma_start(plane[32 * q : 32 * q + 4, :].bitcast(I32), src[0, 4 * q : 4 * q + 4, :].bitcast(I32))
+        def load_plane(plane, src):
+            for quad in range(QUADS):
+                nc.sync.dma_start(
+                    plane[32 * quad : 32 * quad + 4, :].bitcast(I32),
+                    src[0, 4 * quad : 4 * quad + 4, :].bitcast(I32),
+                )
 
-        def words_i32(src):
-            return src[0].rearrange("p n t -> p (n t)").bitcast(I32)
+        def e4m3_words(src):
+            return src[0].rearrange("q c t -> q (c t)").bitcast(I32)
+
+        def deal_slice(copy, dst, src, t):
+            copy(
+                dst[:].rearrange("p (t q) -> p t q", t=PACK)[:, t : t + 1, :],
+                src[:].rearrange("p (q t) -> p t q", t=PACK)[:, t : t + 1, :],
+            )
 
         xt_w = tile("xt_w", T, U16)
         xt_s = tile("xt_s", T, U8)
-        w_raw = tile("w_raw", R, U32)
+        w_w_raw = tile("w_w_raw", R, U32)
         w_s_raw = tile("w_s_raw", R, U8)
-        late_s = tile("late_s", 2 * N + O, U8)
-        wb_s, ws_s, sx_s = late_s[:, 0:N], late_s[:, N : 2 * N], late_s[:, 2 * N : 2 * N + O]
+        second_s = tile("second_s", 2 * N + O, U8)
+        wb_s, ws_s, sx_s = second_s[:, 0:N], second_s[:, N : 2 * N], second_s[:, 2 * N : 2 * N + O]
         wb_w = tile("wb_w", 2 * N, U8)
         ws_w = tile("ws_w", N, U32)
         sx_w = tile("sx_w", O, U32)
-        pages = [tile("page%d" % h, E, F32) for h in range(2)]
+        pages = [tile("page%d" % h, E, F32) for h in range(ROW_TILES)]
 
         nc.vector.memset(xt_s[:, : T // 2].bitcast(I32), 0)
         nc.gpsimd.memset(xt_s[:, T // 2 :].bitcast(I32), 0)
         nc.vector.memset(w_s_raw[:].bitcast(I32), 0)
-        nc.vector.memset(late_s[:].bitcast(I32), 0)
-        for page in pages:
-            nc.vector.memset(page[:], 0.0)
+        nc.vector.memset(second_s[:].bitcast(I32), 0)
 
-        l1 = load_list("l1", offs)
-        l2 = load_list("l2", offs2)
-        for q in range(QUADS):
-            load_scale_rows(nc.sync, xt_s, xt_scales, q)
-        l3 = load_list("l3", offs3)
+        a_tokens = load_list("a_tokens", offs)
+        b_tokens = load_list("b_tokens", offs2)
+        nc.gpsimd.dma_start(w_w_raw[:].bitcast(I32), e4m3_words(w_words))
+        for page in pages:
+            nc.gpsimd.memset(page[:], 0.0)
+        load_plane(xt_s, xt_scales)
+        a_slots = load_list("a_slots", offs3)
         nc.sync.dma_start(xt_w[:].bitcast(I32), xt_words[0].bitcast(I32))
-        nc.sync.dma_start(w_raw[:].bitcast(I32), words_i32(w_words))
-        for q in range(QUADS):
-            load_scale_rows(nc.sync, w_s_raw, w_scales, q)
-        l4 = load_list("l4", offs4)
-        nc.sync.dma_start(ws_w[:].bitcast(I32), words_i32(ws_words))
-        nc.sync.dma_start(sx_w[:].bitcast(I32), words_i32(sx_words))
-        for q in range(QUADS):
-            load_scale_rows(nc.sync, sx_s, sx_scales, q)
-        for q in range(QUADS):
-            load_scale_rows(nc.sync, ws_s, ws_scales, q)
+        load_plane(w_s_raw, w_scales)
+        b_slots = load_list("b_slots", offs4)
+        nc.sync.dma_start(ws_w[:].bitcast(I32), e4m3_words(ws_words))
+        nc.sync.dma_start(sx_w[:].bitcast(I32), e4m3_words(sx_words))
+        load_plane(sx_s, sx_scales)
+        load_plane(ws_s, ws_scales)
         nc.sync.dma_start(wb_w[:].bitcast(I32), wb_words[0].bitcast(I32))
-        for q in range(QUADS):
-            load_scale_rows(nc.sync, wb_s, wb_scales, q)
-        l5 = load_list("l5", offs5)
+        load_plane(wb_s, wb_scales)
+        page_cols = load_list("page_cols", offs5)
 
         w_w = tile("w_w", R, U32)
         w_s = tile("w_s", R, U8)
-        picked_w = [tile("picked_w%d" % i, J, U16) for i in range(2)]
-        picked_s = [tile("picked_s%d" % i, J, U8) for i in range(2)]
+        picked_w = [tile("picked_w%d" % side, J, U16) for side in (A, B)]
+        picked_s = [tile("picked_s%d" % side, J, U8) for side in (A, B)]
 
-        def deal(engine, dst, src, t0, t1):
-            engine(
-                dst[:].rearrange("p (t m) -> p t m", t=PACK)[:, t0:t1, :],
-                src[:].rearrange("p (m t) -> p t m", t=PACK)[:, t0:t1, :],
+        nc.vector.tensor_copy(picked_s[A][:], xt_s[:].indirect(a_tokens[:]))
+        nc.vector.tensor_copy(picked_s[B][:], xt_s[:].indirect(b_tokens[:]))
+        nc.vector.tensor_copy(picked_w[A][:], xt_w[:].indirect(a_tokens[:]))
+        deal_slice(nc.vector.tensor_copy, w_s, w_s_raw, 0)
+        nc.vector.tensor_copy(picked_w[B][:], xt_w[:].indirect(b_tokens[:]))
+        for t in range(PACK):
+            deal_slice(nc.scalar.copy, w_w, w_w_raw, t)
+        for t in range(1, PACK):
+            deal_slice(nc.gpsimd.tensor_copy, w_s, w_s_raw, t)
+
+        banks = [
+            [ps.tile([P, J], F32, name="bank%d%d" % (side, t), tag="bank%d%d" % (side, t)) for t in range(PACK)]
+            for side in (A, B)
+        ]
+
+        def first_stage(side, t):
+            cols = slice(t * P, (t + 1) * P)
+            nc.tensor.matmul_mx(
+                out=banks[side][t][:], lhsT=w_w[:, cols].bitcast(E4M3), lhsT_scale=w_s[:, cols],
+                rhs=picked_w[side][:].bitcast(E2M1), rhs_scale=picked_s[side][:], start=True, stop=True,
             )
 
-        nc.vector.tensor_copy(picked_s[0][:], xt_s[:].indirect(l1[:]))
-        nc.vector.tensor_copy(picked_s[1][:], xt_s[:].indirect(l2[:]))
-        nc.vector.tensor_copy(picked_w[0][:], xt_w[:].indirect(l1[:]))
-        nc.vector.tensor_copy(picked_w[1][:], xt_w[:].indirect(l2[:]))
-        for t in range(PACK):
-            deal(nc.scalar.copy, w_w, w_raw, t, t + 1)
-        deal(nc.vector.tensor_copy, w_s, w_s_raw, 0, 1)
-        deal(nc.vector.tensor_copy, w_s, w_s_raw, 1, PACK)
-
-        banks = [[ps.tile([P, J], F32, name="bank%d%d" % (i, t), tag="bank%d%d" % (i, t)) for t in range(PACK)] for i in range(2)]
-        for t in range(PACK):
-            for i in range(2):
-                cols = slice(t * P, (t + 1) * P)
-                nc.tensor.matmul_mx(
-                    out=banks[i][t][:], lhsT=w_w[:, cols].bitcast(E4M3), lhsT_scale=w_s[:, cols],
-                    rhs=picked_w[i][:].bitcast(E2M1), rhs_scale=picked_s[i][:], start=True, stop=True,
-                )
+        for side in (A, B):
+            for t in range(PACK // 2):
+                first_stage(side, t)
+        for t in range(PACK // 2, PACK):
+            for side in (A, B):
+                first_stage(side, t)
 
         a = [tile("a%d" % t, J, F32) for t in range(PACK)]
         b = [tile("b%d" % t, J, F32) for t in range(PACK)]
-        a_g = sb.tile([P, PACK, O], F32, name="a_g", align_bytes=64)
+        a_picked = sb.tile([P, PACK, O], F32, name="a_picked", align_bytes=64)
         diff = sb.tile([P, PACK, O], F32, name="diff", align_bytes=64)
         hid = sb.tile([P, O, PACK], BF16, name="hid", align_bytes=64)
-        woven = diff[:].rearrange("p t o -> p o t")
+        diff_by_place = diff[:].rearrange("p t o -> p o t")
+
         for t in range(PACK):
-            nc.scalar.activation(a[t][:], banks[0][t][:], ACT.Copy)
+            nc.scalar.activation(a[t][:], banks[A][t][:], ACT.Copy)
             if t == 0:
-                nc.vector.tensor_copy(b[t][:], banks[1][t][:])
+                nc.vector.tensor_copy(b[t][:], banks[B][t][:])
             else:
-                nc.scalar.activation(b[t][:], banks[1][t][:], ACT.Copy)
+                nc.scalar.activation(b[t][:], banks[B][t][:], ACT.Copy)
             if t in (0, PACK - 1):
-                nc.scalar.activation(a_g[:, t, :], a[t][:].indirect(l3[:]), ACT.Copy)
+                nc.scalar.activation(a_picked[:, t, :], a[t][:].indirect(a_slots[:]), ACT.Copy)
             else:
-                nc.vector.tensor_copy(a_g[:, t, :], a[t][:].indirect(l3[:]))
-            nc.vector.tensor_tensor(diff[:, t, :], b[t][:].indirect(l4[:]), a_g[:, t, :], ALU.subtract)
-        for t in range(0, PACK, 2):
-            nc.scalar.activation(hid[:, :, t : t + 2], woven[:, :, t : t + 2], ACT.Abs)
+                nc.vector.tensor_copy(a_picked[:, t, :], a[t][:].indirect(a_slots[:]))
+            nc.vector.tensor_tensor(diff[:, t, :], b[t][:].indirect(b_slots[:]), a_picked[:, t, :], ALU.subtract)
+
+        half = O // 2
+        nc.scalar.activation(hid[:, :, 0:2], diff_by_place[:, :, 0:2], ACT.Abs)
+        nc.scalar.activation(hid[:, :half, 2:4], diff_by_place[:, :half, 2:4], ACT.Abs)
+        last = diff_by_place[:, half:, 2:4]
+        nc.vector.scalar_tensor_tensor(hid[:, half:, 2:4], last, -1.0, last, ALU.mult, ALU.max)
 
         hid_w = tile("hid_w", O, U32)
         hid_s = tile("hid_s", O, U8)
         nc.vector.quantize_mx(out=hid_w[:].bitcast(E5M2), scales=hid_s[:], in_=hid[:].rearrange("p o t -> p (o t)"))
 
-        acc = [ps.tile([P, O], F32, name="acc%d" % h, tag="bank0%d" % h) for h in range(2)]
-        for h in range(2):
+        acc = [ps.tile([P, O], F32, name="acc%d" % h, tag="bank%d%d" % (A, h)) for h in range(ROW_TILES)]
+        for h in range(ROW_TILES):
             cols = slice(h * P, (h + 1) * P)
             nc.tensor.matmul_mx(
                 out=acc[h][:], lhsT=ws_w[:, cols].bitcast(E4M3), lhsT_scale=ws_s[:, cols],
                 rhs=sx_w[:].bitcast(E4M3), rhs_scale=sx_s, start=True, stop=False,
             )
-        for h in range(2):
+        for h in range(ROW_TILES):
             cols = slice(h * P, (h + 1) * P)
+            byte_cols = slice(2 * h * P, 2 * (h + 1) * P)
             nc.tensor.matmul_mx(
-                out=acc[h][:], lhsT=wb_w[:, 2 * h * P : 2 * (h + 1) * P].bitcast(E2M1), lhsT_scale=wb_s[:, cols],
+                out=acc[h][:], lhsT=wb_w[:, byte_cols].bitcast(E2M1), lhsT_scale=wb_s[:, cols],
                 rhs=hid_w[:].bitcast(E5M2), rhs_scale=hid_s[:], start=False, stop=True,
             )
 
-        p_sb = [tile("p%d" % h, O, F32) for h in range(2)]
-        nc.vector.tensor_copy(p_sb[0][:], acc[0][:])
-        nc.scalar.activation(p_sb[1][:], acc[1][:], ACT.Copy)
-        nc.vector.tensor_copy(pages[0][:].indirect(l5[:]), p_sb[0][:])
-        nc.scalar.activation(pages[1][:].indirect(l5[:]), p_sb[1][:], ACT.Copy)
+        p_rows = [tile("p%d" % h, O, F32) for h in range(ROW_TILES)]
+        nc.vector.tensor_copy(p_rows[0][:], acc[0][:])
+        nc.scalar.activation(p_rows[1][:], acc[1][:], ACT.Copy)
+        nc.vector.tensor_copy(pages[0][:].indirect(page_cols[:]), p_rows[0][:])
+        nc.scalar.activation(pages[1][:].indirect(page_cols[:]), p_rows[1][:], ACT.Copy)
         nc.sync.dma_start(out[0:P, :], pages[0][:])
         nc.scalar.dma_start(out[P : 2 * P, :], pages[1][:])

@@ -51,10 +51,10 @@ def tile_list_tied_looked_skip_scattered_kernel(
         def e4m3_words(src):
             return src[0].rearrange("q c t -> q (c t)").bitcast(I32)
 
-        def deal_slice(copy, dst, src, t):
+        def deal_slices(copy, dst, src, t0, t1):
             copy(
-                dst[:].rearrange("p (t q) -> p t q", t=PACK)[:, t : t + 1, :],
-                src[:].rearrange("p (q t) -> p t q", t=PACK)[:, t : t + 1, :],
+                dst[:].rearrange("p (t q) -> p t q", t=PACK)[:, t0:t1, :],
+                src[:].rearrange("p (q t) -> p t q", t=PACK)[:, t0:t1, :],
             )
 
         xt_w = tile("xt_w", T, U16)
@@ -75,12 +75,12 @@ def tile_list_tied_looked_skip_scattered_kernel(
 
         a_tokens = load_list("a_tokens", offs)
         b_tokens = load_list("b_tokens", offs2)
-        nc.gpsimd.dma_start(w_w_raw[:].bitcast(I32), e4m3_words(w_words))
         for page in pages:
-            nc.gpsimd.memset(page[:], 0.0)
+            nc.vector.memset(page[:], 0.0)
         load_plane(xt_s, xt_scales)
         a_slots = load_list("a_slots", offs3)
         nc.sync.dma_start(xt_w[:].bitcast(I32), xt_words[0].bitcast(I32))
+        nc.sync.dma_start(w_w_raw[:].bitcast(I32), e4m3_words(w_words))
         load_plane(w_s_raw, w_scales)
         b_slots = load_list("b_slots", offs4)
         nc.sync.dma_start(ws_w[:].bitcast(I32), e4m3_words(ws_words))
@@ -99,12 +99,11 @@ def tile_list_tied_looked_skip_scattered_kernel(
         nc.vector.tensor_copy(picked_s[A][:], xt_s[:].indirect(a_tokens[:]))
         nc.vector.tensor_copy(picked_s[B][:], xt_s[:].indirect(b_tokens[:]))
         nc.vector.tensor_copy(picked_w[A][:], xt_w[:].indirect(a_tokens[:]))
-        deal_slice(nc.vector.tensor_copy, w_s, w_s_raw, 0)
         nc.vector.tensor_copy(picked_w[B][:], xt_w[:].indirect(b_tokens[:]))
+        deal_slices(nc.vector.tensor_copy, w_s, w_s_raw, 0, PACK // 2)
+        deal_slices(nc.vector.tensor_copy, w_s, w_s_raw, PACK // 2, PACK)
         for t in range(PACK):
-            deal_slice(nc.scalar.copy, w_w, w_w_raw, t)
-        for t in range(1, PACK):
-            deal_slice(nc.gpsimd.tensor_copy, w_s, w_s_raw, t)
+            deal_slices(nc.scalar.copy, w_w, w_w_raw, t, t + 1)
 
         banks = [
             [ps.tile([P, J], F32, name="bank%d%d" % (side, t), tag="bank%d%d" % (side, t)) for t in range(PACK)]

from contextlib import ExitStack

import concourse.mybir as mybir

K, T, J, R, O, N, L, E = 512, 2048, 256, 512, 128, 256, 512, 1024
FLOPS = 2 * (2 * K * R * J + R * N * O + L * N * O)

F32 = mybir.dt.float32
BF16 = mybir.dt.bfloat16
I32 = mybir.dt.int32
U32 = mybir.dt.uint32
U16 = mybir.dt.uint16
U8 = mybir.dt.uint8
E4M3 = mybir.dt.float8_e4m3fn_x4
E5M2 = mybir.dt.float8_e5m2_x4
E2M1 = mybir.dt.float4_e2m1fn_x4
ACT = mybir.ActivationFunctionType
ALU = mybir.AluOpType

P = 128
PACK = 4
QUADS = 4
ROW_TILES = N // P
A, B = 0, 1


def tile_list_tied_looked_skip_scattered_kernel(
    tc, xt_words, xt_scales, w_words, w_scales, wb_words, wb_scales, sx_words, sx_scales,
    ws_words, ws_scales, offs, offs2, offs3, offs4, offs5, out,
):
    nc = tc.nc
    with ExitStack() as ctx:
        sb = ctx.enter_context(tc.tile_pool(name="sb", bufs=1))
        ps = ctx.enter_context(tc.psum_pool(name="ps", bufs=1))

        def tile(name, cols, dtype):
            return sb.tile([P, cols], dtype, name=name, align_bytes=64)

        def load_list(name, src):
            offsets = tile(name, src.shape[1], U16)
            nc.sync.dma_start(offsets[:], src)
            return offsets

        def load_plane(plane, src):
            for quad in range(QUADS):
                nc.sync.dma_start(
                    plane[32 * quad : 32 * quad + 4, :].bitcast(I32),
                    src[0, 4 * quad : 4 * quad + 4, :].bitcast(I32),
                )

        def e4m3_words(src):
            return src[0].rearrange("q c t -> q (c t)").bitcast(I32)

        def deal_slices(copy, dst, src, t0, t1):
            copy(
                dst[:].rearrange("p (t q) -> p t q", t=PACK)[:, t0:t1, :],
                src[:].rearrange("p (q t) -> p t q", t=PACK)[:, t0:t1, :],
            )

        xt_w = tile("xt_w", T, U16)
        xt_s = tile("xt_s", T, U8)
        w_w_raw = tile("w_w_raw", R, U32)
        w_s_raw = tile("w_s_raw", R, U8)
        second_s = tile("second_s", 2 * N + O, U8)
        wb_s, ws_s, sx_s = second_s[:, 0:N], second_s[:, N : 2 * N], second_s[:, 2 * N : 2 * N + O]
        wb_w = tile("wb_w", 2 * N, U8)
        ws_w = tile("ws_w", N, U32)
        sx_w = tile("sx_w", O, U32)
        pages = [tile("page%d" % h, E, F32) for h in range(ROW_TILES)]

        nc.vector.memset(xt_s[:, : T // 2].bitcast(I32), 0)
        nc.gpsimd.memset(xt_s[:, T // 2 :].bitcast(I32), 0)
        nc.vector.memset(w_s_raw[:].bitcast(I32), 0)
        nc.vector.memset(second_s[:].bitcast(I32), 0)

        a_tokens = load_list("a_tokens", offs)
        b_tokens = load_list("b_tokens", offs2)
        for page in pages:
            nc.vector.memset(page[:], 0.0)
        load_plane(xt_s, xt_scales)
        a_slots = load_list("a_slots", offs3)
        nc.sync.dma_start(xt_w[:].bitcast(I32), xt_words[0].bitcast(I32))
        nc.sync.dma_start(w_w_raw[:].bitcast(I32), e4m3_words(w_words))
        load_plane(w_s_raw, w_scales)
        b_slots = load_list("b_slots", offs4)
        nc.sync.dma_start(ws_w[:].bitcast(I32), e4m3_words(ws_words))
        nc.sync.dma_start(sx_w[:].bitcast(I32), e4m3_words(sx_words))
        load_plane(sx_s, sx_scales)
        load_plane(ws_s, ws_scales)
        nc.sync.dma_start(wb_w[:].bitcast(I32), wb_words[0].bitcast(I32))
        load_plane(wb_s, wb_scales)
        page_cols = load_list("page_cols", offs5)

        w_w = tile("w_w", R, U32)
        w_s = tile("w_s", R, U8)
        picked_w = [tile("picked_w%d" % side, J, U16) for side in (A, B)]
        picked_s = [tile("picked_s%d" % side, J, U8) for side in (A, B)]

        nc.vector.tensor_copy(picked_s[A][:], xt_s[:].indirect(a_tokens[:]))
        nc.vector.tensor_copy(picked_s[B][:], xt_s[:].indirect(b_tokens[:]))
        nc.vector.tensor_copy(picked_w[A][:], xt_w[:].indirect(a_tokens[:]))
        nc.vector.tensor_copy(picked_w[B][:], xt_w[:].indirect(b_tokens[:]))
        deal_slices(nc.vector.tensor_copy, w_s, w_s_raw, 0, PACK // 2)
        deal_slices(nc.vector.tensor_copy, w_s, w_s_raw, PACK // 2, PACK)
        for t in range(PACK):
            deal_slices(nc.scalar.copy, w_w, w_w_raw, t, t + 1)

        banks = [
            [ps.tile([P, J], F32, name="bank%d%d" % (side, t), tag="bank%d%d" % (side, t)) for t in range(PACK)]
            for side in (A, B)
        ]

        def first_stage(side, t):
            cols = slice(t * P, (t + 1) * P)
            nc.tensor.matmul_mx(
                out=banks[side][t][:], lhsT=w_w[:, cols].bitcast(E4M3), lhsT_scale=w_s[:, cols],
                rhs=picked_w[side][:].bitcast(E2M1), rhs_scale=picked_s[side][:], start=True, stop=True,
            )

        for side in (A, B):
            for t in range(PACK // 2):
                first_stage(side, t)
        for t in range(PACK // 2, PACK):
            for side in (A, B):
                first_stage(side, t)

        a = [tile("a%d" % t, J, F32) for t in range(PACK)]
        b = [tile("b%d" % t, J, F32) for t in range(PACK)]
        a_picked = sb.tile([P, PACK, O], F32, name="a_picked", align_bytes=64)
        diff = sb.tile([P, PACK, O], F32, name="diff", align_bytes=64)
        hid = sb.tile([P, O, PACK], BF16, name="hid", align_bytes=64)
        diff_by_place = diff[:].rearrange("p t o -> p o t")

        for t in range(PACK):
            nc.scalar.activation(a[t][:], banks[A][t][:], ACT.Copy)
            if t == 0:
                nc.vector.tensor_copy(b[t][:], banks[B][t][:])
            else:
                nc.scalar.activation(b[t][:], banks[B][t][:], ACT.Copy)
            if t in (0, PACK - 1):
                nc.scalar.activation(a_picked[:, t, :], a[t][:].indirect(a_slots[:]), ACT.Copy)
            else:
                nc.vector.tensor_copy(a_picked[:, t, :], a[t][:].indirect(a_slots[:]))
            nc.vector.tensor_tensor(diff[:, t, :], b[t][:].indirect(b_slots[:]), a_picked[:, t, :], ALU.subtract)

        half = O // 2
        nc.scalar.activation(hid[:, :, 0:2], diff_by_place[:, :, 0:2], ACT.Abs)
        nc.scalar.activation(hid[:, :half, 2:4], diff_by_place[:, :half, 2:4], ACT.Abs)
        last = diff_by_place[:, half:, 2:4]
        nc.vector.scalar_tensor_tensor(hid[:, half:, 2:4], last, -1.0, last, ALU.mult, ALU.max)

        hid_w = tile("hid_w", O, U32)
        hid_s = tile("hid_s", O, U8)
        nc.vector.quantize_mx(out=hid_w[:].bitcast(E5M2), scales=hid_s[:], in_=hid[:].rearrange("p o t -> p (o t)"))

        acc = [ps.tile([P, O], F32, name="acc%d" % h, tag="bank%d%d" % (A, h)) for h in range(ROW_TILES)]
        for h in range(ROW_TILES):
            cols = slice(h * P, (h + 1) * P)
            nc.tensor.matmul_mx(
                out=acc[h][:], lhsT=ws_w[:, cols].bitcast(E4M3), lhsT_scale=ws_s[:, cols],
                rhs=sx_w[:].bitcast(E4M3), rhs_scale=sx_s, start=True, stop=False,
            )
        for h in range(ROW_TILES):
            cols = slice(h * P, (h + 1) * P)
            byte_cols = slice(2 * h * P, 2 * (h + 1) * P)
            nc.tensor.matmul_mx(
                out=acc[h][:], lhsT=wb_w[:, byte_cols].bitcast(E2M1), lhsT_scale=wb_s[:, cols],
                rhs=hid_w[:].bitcast(E5M2), rhs_scale=hid_s[:], start=False, stop=True,
            )

        p_rows = [tile("p%d" % h, O, F32) for h in range(ROW_TILES)]
        nc.vector.tensor_copy(p_rows[0][:], acc[0][:])
        nc.scalar.activation(p_rows[1][:], acc[1][:], ACT.Copy)
        nc.vector.tensor_copy(pages[0][:].indirect(page_cols[:]), p_rows[0][:])
        nc.scalar.activation(pages[1][:].indirect(page_cols[:]), p_rows[1][:], ACT.Copy)
        nc.sync.dma_start(out[0:P, :], pages[0][:])
        nc.scalar.dma_start(out[P : 2 * P, :], pages[1][:])
